import numpy as np
import ml_dtypes


def mxq(x, axis, fmt="e4m3"):
    dtype, down = {"e4m3": (ml_dtypes.float8_e4m3fn, 7), "e5m2": (ml_dtypes.float8_e5m2, 14)}[fmt]
    v = np.moveaxis(np.asarray(x, np.float32).astype(ml_dtypes.bfloat16).astype(np.float64), axis, -1)
    blocks = v.reshape(v.shape[:-1] + (-1, 32))
    amax = np.abs(blocks).max(-1, keepdims=True)
    byte = np.maximum(np.where(amax > 0, np.frexp(amax)[1] - 1 + 127, 0) - down, 1)
    scale = np.exp2(byte - 127.0)
    codes = (blocks / scale).astype(np.float32).astype(dtype).astype(np.float64)
    return np.moveaxis((codes * scale).reshape(v.shape), -1, axis)


WIDE = False


def mx_kscale(k):
    if not WIDE:
        return np.ones(k)
    levels = np.array([10, -10, 5, -5, 0])
    if k % 512:
        return np.exp2(np.random.permutation(np.resize(levels, k // 32))).repeat(32)
    a = np.empty((k // 512, 16))
    for p in range(k // 512):
        a[p, :8] = np.random.permutation(np.resize(levels, 8))
        for g in range(8):
            far = levels[np.abs(levels - a[p, g]) >= 10]
            a[p, g + 8] = far[np.random.randint(len(far))]
    return np.exp2(a.ravel()).repeat(32)


def f64(x):
    return np.asarray(x).astype(np.float64)


def striped(idx):
    return np.tile(idx.reshape(-1, 16).T, (8, 1)).astype(np.uint16)


def unstriped(offs):
    return offs[:16].T.reshape(-1).astype(np.int64)


def striped8(idx):
    return np.concatenate([x.reshape(-1, 16).T for x in idx]).astype(np.uint16)


def runs(offs, k):
    lists = np.stack([offs[16 * r : 16 * r + 16].T.reshape(-1) for r in range(8)]).astype(np.int64)
    return lists[np.arange(k) % 512 // 64]


def pack_weight(w):
    k, n = w.shape
    w = f64(np.asarray(w, np.float32).astype(ml_dtypes.bfloat16)).reshape(k // 32, 32, n)
    amax = np.abs(w).max(1)
    byte = np.clip(np.where(amax > 0, np.frexp(amax)[1] - 1 + 127 - 7, 1), 1, 254)
    scaled = (w * np.exp2(127.0 - byte)[:, None, :]).reshape(k, n).astype(np.float32)
    words = np.ascontiguousarray(scaled.reshape(k // 512, 128, 4, n).transpose(0, 1, 3, 2)).astype(ml_dtypes.float8_e4m3fn).view(np.uint8)
    return words, np.ascontiguousarray(byte.astype(np.uint8).reshape(k // 512, 16, n))


def unpack_weight(words, scales):
    g, p, n, _ = words.shape
    vals = np.ascontiguousarray(words).view(ml_dtypes.float8_e4m3fn).astype(np.float64) * np.repeat(np.exp2(scales.astype(np.float64) - 127.0), 8, axis=1)[..., None]
    return vals.transpose(0, 1, 3, 2).reshape(g * 512, n)


def sigmoid(v):
    return 1.0 / (1.0 + np.exp(-np.maximum(v, -700.0)))


K, T, S, G, H, W = 512, 1024, 256, 2048, 512, 128


def setup_inputs():
    n = np.random.standard_normal
    s = mx_kscale(K)[:, None]
    packed_xT = pack_weight(n((K, T)) * s)
    packed_dT = pack_weight(n((K, G)) / s)
    perm = np.random.permutation(S)
    return {
        "x_words": packed_xT[0],
        "x_scales": packed_xT[1],
        "d_words": packed_dT[0],
        "d_scales": packed_dT[1],
        "gs": (np.random.uniform(0.5, 1.5, (K, 1)) * s).astype(np.float32),
        "sl": np.random.uniform(1.0, 2.0, (H, 1)).astype(np.float32),
        "th": (0.5 * n((H, 1))).astype(np.float32),
        "offs": striped8(np.random.randint(0, T, (8, S))),
        "k1": striped8(np.random.randint(0, G, (8, H))),
        "n1": striped(perm[:W]),
        "n2": striped(perm[W:]),
        "n3": striped(np.random.permutation(S)),
        "k2": striped8(np.random.randint(0, G, (8, H))),
        "n4": striped(np.random.permutation(S)),
        "n5": striped(np.random.permutation(S)),
    }


def reference(x_words, x_scales, d_words, d_scales, gs, sl, th, offs, k1, n1, n2, n3, k2, n4, n5):
    d_k2 = unpack_weight(d_words, d_scales)[np.arange(K)[:, None], runs(k2, K)]
    d_k1 = unpack_weight(d_words, d_scales)[np.arange(K)[:, None], runs(k1, K)]
    xq = unpack_weight(x_words, x_scales)[np.arange(K)[:, None], runs(offs, K)]
    h = 0.0625 * (d_k1.T @ xq)
    pa = h[:, unstriped(n1)]
    pb = h[:, unstriped(n2)]
    rb = pa - pb
    ds = np.zeros((H, S))
    ds[:, unstriped(n1)] = pb
    dt = ds.copy()
    dt[:, unstriped(n2)] = rb
    z = f64(gs) * (np.maximum(dt, 0.5 * dt[:, unstriped(n3)]))
    h2 = 0.0625 * ((d_k2.T @ mxq(z, 0, "e4m3")))
    ds2 = np.zeros((H, S))
    ds2[:, unstriped(n4)] = h2
    sg = sigmoid(f64(sl) * (ds2[:, unstriped(n5)] - f64(th)))
    return h2 * sg

@@ -1,0 +1,221 @@
+from contextlib import ExitStack
+
+import concourse.mybir as mybir
+
+F32 = mybir.dt.float32
+BF16 = mybir.dt.bfloat16
+I32 = mybir.dt.int32
+U32 = mybir.dt.uint32
+U16 = mybir.dt.uint16
+U8 = mybir.dt.uint8
+FP8X4 = mybir.dt.float8_e4m3fn_x4
+ALU = mybir.AluOpType
+ACT = mybir.ActivationFunctionType
+
+P = 128
+PACK = 4
+K, T, S, G, H = 512, 1024, 256, 2048, 512
+HALF = S // 2
+LIST_COL = 16
+ROW_STEP = 8
+QUAD = 32
+FLOPS = 2 * 2 * K * H * S
+
+
+def tile_picked_hcodeswapderl_none_p_kernel(
+    tc, x_words, x_scales, d_words, d_scales, gs, sl, th, offs, k1, n1, n2, n3, k2, n4, n5, out
+):
+    nc = tc.nc
+    with ExitStack() as ctx:
+        keep = ctx.enter_context(tc.tile_pool(name="keep", bufs=1))
+        psum = ctx.enter_context(tc.psum_pool(name="psum", bufs=1))
+
+        def sb(name, shape, dtype, tag=None):
+            return keep.tile(shape, dtype, name=name, tag=tag or name, align_bytes=64)
+
+        def load_list(name, src):
+            lst = keep.tile(list(src.shape), U16, name=name)
+            nc.sync.dma_start(out=lst[:], in_=src)
+            return lst
+
+        def load_scales(name, src, cols):
+            win = sb(name, [P, cols], U8)
+            rows = src[0].bitcast(I32).unsqueeze(1).to_broadcast([16, ROW_STEP, cols // 4])
+            nc.sync.dma_start(out=win[:].bitcast(I32), in_=rows)
+            return win
+
+        def load_words(name, src, cols):
+            win = sb(name, [P, cols], U32)
+            nc.sync.dma_start(out=win[:].bitcast(I32), in_=src[0].rearrange("p c r -> p (c r)").bitcast(I32))
+            return win
+
+        def load_rows(name, src):
+            col = sb(name, [P, PACK], F32)
+            nc.sync.dma_start(out=col[:], in_=src.rearrange("(p t) o -> p (t o)", t=PACK))
+            return col
+
+        def half_of(lst, c):
+            w = HALF // LIST_COL
+            return lst[:, c * w : (c + 1) * w]
+
+        def place_scales(name, got, cols):
+            plane = sb(name, [P, cols], U8)
+            nc.vector.memset(plane[:].bitcast(I32), 0)
+            for q in range(P // QUAD):
+                nc.scalar.dma_start(
+                    out=plane[QUAD * q : QUAD * q + 4, :].bitcast(I32),
+                    in_=got[QUAD * q : QUAD * (q + 1) : ROW_STEP, :].bitcast(I32),
+                )
+            return plane
+
+        def deal(name, src, dtype, tag=None):
+            dealt = sb(name, [P, H], dtype, tag)
+            nc.vector.tensor_copy(
+                out=dealt[:].rearrange("p (t m) -> p t m", t=PACK), in_=src.rearrange("p (m t) -> p t m", t=PACK)
+            )
+            return dealt
+
+        k1_l = load_list("k1_l", k1)
+        offs_l = load_list("offs_l", offs)
+        d_bytes = load_scales("d_bytes", d_scales, G)
+        x_bytes = load_scales("x_bytes", x_scales, T)
+        d_win = load_words("d_win", d_words, G)
+        x_win = load_words("x_win", x_words, T)
+        n2_l = load_list("n2_l", n2)
+        n1_l = load_list("n1_l", n1)
+        n3_l = load_list("n3_l", n3)
+        k2_l = load_list("k2_l", k2)
+        n4_l = load_list("n4_l", n4)
+        n5_l = load_list("n5_l", n5)
+        gs_c = load_rows("gs_c", gs)
+        sl_c = load_rows("sl_c", sl)
+        th_c = load_rows("th_c", th)
+
+        got1 = sb("got1", [P, H + S], U8)
+        nc.vector.tensor_copy(out=got1[:, :H], in_=d_bytes[:].indirect(k1_l[:]))
+        nc.vector.tensor_copy(out=got1[:, H:], in_=x_bytes[:].indirect(offs_l[:]))
+        plane1 = place_scales("plane1", got1, H + S)
+        w1_got = sb("w1_got", [P, H], U32)
+        nc.vector.tensor_copy(out=w1_got[:], in_=d_win[:].indirect(k1_l[:]))
+        w1 = deal("w1", w1_got[:], U32)
+        xq = sb("xq", [P, S], U32)
+        nc.vector.tensor_copy(out=xq[:], in_=x_win[:].indirect(offs_l[:]))
+        w1_s = deal("w1_s", plane1[:, :H], U8)
+
+        h = []
+        for t in range(PACK):
+            acc = psum.tile([P, S], F32, name=f"acc1_{t}", tag=f"bank{t}")
+            cols = slice(t * P, (t + 1) * P)
+            nc.tensor.matmul_mx(
+                out=acc[:], lhsT=w1[:, cols].bitcast(FP8X4), lhsT_scale=w1_s[:, cols],
+                rhs=xq[:].bitcast(FP8X4), rhs_scale=plane1[:, H:], start=True, stop=True,
+            )
+            h_t = sb(f"h{t}", [P, S], F32)
+            nc.vector.tensor_scalar_mul(h_t[:], acc[:], 0.0625)
+            h.append(h_t)
+
+        bias = sb("bias", [P, PACK], F32)
+        nc.vector.scalar_tensor_tensor(out=bias[:], in0=sl_c[:], scalar=-1.0, in1=th_c[:], op0=ALU.mult, op1=ALU.mult)
+
+        dt = [sb(f"dt{t}", [P, S], F32) for t in range(PACK)]
+        pb = [sb(f"pb{t}", [P, HALF], F32) for t in range(PACK)]
+        rb = [sb(f"rb{t}", [P, HALF], F32) for t in range(PACK)]
+        zb = [sb(f"zb{c}", [P, HALF, PACK], BF16) for c in range(2)]
+
+        def fetch_pair(t):
+            pa = sb(f"pa{t}", [P, HALF], F32)
+            nc.scalar.activation(pb[t][:], h[t][:].indirect(n2_l[:]), ACT.Copy)
+            nc.scalar.activation(pa[:], h[t][:].indirect(n1_l[:]), ACT.Copy)
+            nc.vector.tensor_sub(rb[t][:], pa[:], pb[t][:])
+
+        def put_pb(t):
+            nc.scalar.activation(dt[t][:].indirect(n1_l[:]), pb[t][:], ACT.Copy)
+
+        def put_rb(t):
+            nc.scalar.activation(dt[t][:].indirect(n2_l[:]), rb[t][:], ACT.Copy)
+
+        def make_z(t, c, other, big):
+            nc.scalar.activation(other, dt[t][:].indirect(half_of(n3_l, c)), ACT.Copy)
+            nc.vector.scalar_tensor_tensor(
+                out=big, in0=other, scalar=0.5, in1=dt[t][:, c * HALF : (c + 1) * HALF], op0=ALU.mult, op1=ALU.max
+            )
+            nc.vector.tensor_scalar_mul(zb[c][:, :, t], big, gs_c[:, t : t + 1])
+
+        early = sb("early", [P, PACK, HALF], F32)
+        big0 = sb("big0", [P, PACK, HALF], F32)
+        fetch_pair(0)
+        got2 = sb("got2", [P, H], U8)
+        nc.vector.tensor_copy(out=got2[:], in_=d_bytes[:].indirect(k2_l[:]))
+        plane2 = sb("plane2", [P, H], U8)
+        nc.vector.memset(plane2[:].bitcast(I32), 0)
+        for q in range(P // QUAD):
+            nc.sync.dma_start(
+                out=plane2[QUAD * q : QUAD * q + 4, :].bitcast(I32),
+                in_=got2[QUAD * q : QUAD * (q + 1) : ROW_STEP, :].bitcast(I32),
+            )
+        w2_s = deal("w2_s", plane2[:], U8, tag="pa0")
+        put_pb(0)
+        fetch_pair(1)
+        w2_got = sb("w2_got", [P, H], U32, tag="pa1")
+        nc.vector.tensor_copy(out=w2_got[:], in_=d_win[:].indirect(k2_l[:]))
+        w2 = deal("w2", w2_got[:], U32)
+        put_rb(0)
+        put_pb(1)
+        make_z(0, 0, early[:, 0, :], big0[:, 0, :])
+        for t in range(2, PACK):
+            fetch_pair(t)
+            put_rb(t - 1)
+            put_pb(t)
+            make_z(t - 1, 0, early[:, t - 1, :], big0[:, t - 1, :])
+        put_rb(PACK - 1)
+        make_z(PACK - 1, 0, early[:, PACK - 1, :], big0[:, PACK - 1, :])
+
+        h2 = [sb(f"h2_{t}", [P, S], F32) for t in range(PACK)]
+        ds2 = [sb(f"ds2_{t}", [P, 2 * S], F32) for t in range(PACK)]
+
+        def second_product(c):
+            codes = sb(f"z_codes{c}", [P, HALF], U32)
+            scales = sb(f"z_scales{c}", [P, HALF], U8)
+            nc.vector.quantize_mx(
+                out=codes[:].bitcast(FP8X4), scales=scales[:], in_=zb[c][:].rearrange("p j t -> p (j t)")
+            )
+            for t in range(PACK):
+                acc = psum.tile([P, HALF], F32, name=f"acc2_{t}_{c}", tag=f"bank{PACK * (1 - c) + t}")
+                cols = slice(t * P, (t + 1) * P)
+                nc.tensor.matmul_mx(
+                    out=acc[:], lhsT=w2[:, cols].bitcast(FP8X4), lhsT_scale=w2_s[:, cols],
+                    rhs=codes[:].bitcast(FP8X4), rhs_scale=scales[:], start=True, stop=True,
+                )
+                nc.vector.tensor_scalar_mul(h2[t][:, c * HALF : (c + 1) * HALF], acc[:], 0.0625)
+
+        def put_h2(t, c):
+            nc.scalar.activation(ds2[t][:].indirect(half_of(n4_l, c)), h2[t][:, c * HALF : (c + 1) * HALF], ACT.Copy)
+
+        out_rows = out.rearrange("(p t) j -> p t j", t=PACK)
+
+        def finish(t, pieces):
+            w = S // pieces
+            for c in range(pieces):
+                cols = slice(c * w, (c + 1) * w)
+                sg = sb(f"sg{t}_{c}", [P, w], F32)
+                nc.scalar.activation(
+                    sg[:], ds2[t][:].indirect(n5_l[:, c * w // LIST_COL : (c + 1) * w // LIST_COL]), ACT.Sigmoid,
+                    bias=bias[:, t : t + 1], scale=sl_c[:, t : t + 1],
+                )
+                res = sb(f"res{t}_{c}", [P, w], F32)
+                nc.vector.tensor_mul(res[:], h2[t][:, cols], sg[:])
+                nc.sync.dma_start(out=out_rows[:, t, cols], in_=res[:])
+
+        second_product(0)
+        late = sb("late", [P, PACK, HALF], F32, tag=f"rb{PACK - 1}")
+        big1 = sb("big1", [P, PACK, HALF], F32, tag="zb0")
+        for t in range(PACK):
+            make_z(t, 1, late[:, t, :], big1[:, t, :])
+        second_product(1)
+        for t in range(PACK):
+            put_h2(t, 0)
+        put_h2(0, 1)
+        for t in range(1, PACK):
+            put_h2(t, 1)
+            finish(t - 1, 1)
+        finish(PACK - 1, 2)

@@ -75,6 +75,10 @@ def tile_picked_hcodeswapderl_none_p_kernel(
             )
             return dealt
 
+        warm = sb("warm", [P, 16], F32)
+        nc.gpsimd.memset(warm[:, 0:1], 0.0)
+        nc.scalar.activation(warm[:, 8:9], warm[:, 0:1], ACT.Sigmoid)
+
         k1_l = load_list("k1_l", k1)
         offs_l = load_list("offs_l", offs)
         d_bytes = load_scales("d_bytes", d_scales, G)

@@ -70,8 +70,10 @@ def tile_picked_hcodeswapderl_none_p_kernel(
 
         def deal(name, src, dtype, tag=None):
             dealt = sb(name, [P, H], dtype, tag)
+            run = 16 if dtype == U8 else 4
             nc.vector.tensor_copy(
-                out=dealt[:].rearrange("p (t m) -> p t m", t=PACK), in_=src.rearrange("p (m t) -> p t m", t=PACK)
+                out=dealt[:].rearrange("p (t a b) -> p a t b", t=PACK, b=run),
+                in_=src.rearrange("p (a b t) -> p a t b", t=PACK, b=run),
             )
             return dealt
 
@@ -104,7 +106,7 @@ def tile_picked_hcodeswapderl_none_p_kernel(
         w1 = deal("w1", w1_got[:], U32)
         xq = sb("xq", [P, S], U32)
         nc.vector.tensor_copy(out=xq[:], in_=x_win[:].indirect(offs_l[:]))
-        w1_s = deal("w1_s", plane1[:, :H], U8)
+        w1_s = deal("w1_s", plane1[:, :H], U8, tag="x_win")
 
         h = []
         for t in range(PACK):
@@ -124,7 +126,6 @@ def tile_picked_hcodeswapderl_none_p_kernel(
         dt = [sb(f"dt{t}", [P, S], F32) for t in range(PACK)]
         pb = [sb(f"pb{t}", [P, HALF], F32) for t in range(PACK)]
         rb = [sb(f"rb{t}", [P, HALF], F32) for t in range(PACK)]
-        zb = [sb(f"zb{c}", [P, HALF, PACK], BF16) for c in range(2)]
 
         def fetch_pair(t):
             pa = sb(f"pa{t}", [P, HALF], F32)
@@ -146,9 +147,8 @@ def tile_picked_hcodeswapderl_none_p_kernel(
             nc.vector.tensor_scalar_mul(zb[c][:, :, t], big, gs_c[:, t : t + 1])
 
         early = sb("early", [P, PACK, HALF], F32)
-        big0 = sb("big0", [P, PACK, HALF], F32)
         fetch_pair(0)
-        got2 = sb("got2", [P, H], U8)
+        got2 = sb("got2", [P, H], U8, tag="pa0")
         nc.vector.tensor_copy(out=got2[:], in_=d_bytes[:].indirect(k2_l[:]))
         plane2 = sb("plane2", [P, H], U8)
         nc.vector.memset(plane2[:].bitcast(I32), 0)
@@ -157,12 +157,14 @@ def tile_picked_hcodeswapderl_none_p_kernel(
                 out=plane2[QUAD * q : QUAD * q + 4, :].bitcast(I32),
                 in_=got2[QUAD * q : QUAD * (q + 1) : ROW_STEP, :].bitcast(I32),
             )
-        w2_s = deal("w2_s", plane2[:], U8, tag="pa0")
+        w2_s = deal("w2_s", plane2[:], U8)
+        big0 = sb("big0", [P, PACK, HALF], F32, tag="plane2")
         put_pb(0)
         fetch_pair(1)
         w2_got = sb("w2_got", [P, H], U32, tag="pa1")
         nc.vector.tensor_copy(out=w2_got[:], in_=d_win[:].indirect(k2_l[:]))
         w2 = deal("w2", w2_got[:], U32)
+        zb = [sb("zb0", [P, HALF, PACK], BF16, tag="pa1"), sb("zb1", [P, HALF, PACK], BF16)]
         put_rb(0)
         put_pb(1)
         make_z(0, 0, early[:, 0, :], big0[:, 0, :])
@@ -212,7 +214,7 @@ def tile_picked_hcodeswapderl_none_p_kernel(
 
         second_product(0)
         late = sb("late", [P, PACK, HALF], F32, tag=f"rb{PACK - 1}")
-        big1 = sb("big1", [P, PACK, HALF], F32, tag="zb0")
+        big1 = sb("big1", [P, PACK, HALF], F32, tag="pa1")
         for t in range(PACK):
             make_z(t, 1, late[:, t, :], big1[:, t, :])
         second_product(1)

@@ -44,8 +44,7 @@ def tile_picked_hcodeswapderl_none_p_kernel(
             nc.sync.dma_start(out=win[:].bitcast(I32), in_=rows)
             return win
 
-        def load_words(name, src, cols):
-            win = sb(name, [P, cols], U32)
+        def load_words(win, src):
             nc.sync.dma_start(out=win[:].bitcast(I32), in_=src[0].rearrange("p c r -> p (c r)").bitcast(I32))
             return win
 
@@ -81,12 +80,12 @@ def tile_picked_hcodeswapderl_none_p_kernel(
         nc.gpsimd.memset(warm[:, 0:1], 0.0)
         nc.scalar.activation(warm[:, 8:9], warm[:, 0:1], ACT.Sigmoid)
 
-        k1_l = load_list("k1_l", k1)
+        x_bytes = load_scales("x_bytes", x_scales, T)
         offs_l = load_list("offs_l", offs)
         d_bytes = load_scales("d_bytes", d_scales, G)
-        x_bytes = load_scales("x_bytes", x_scales, T)
-        d_win = load_words("d_win", d_words, G)
-        x_win = load_words("x_win", x_words, T)
+        k1_l = load_list("k1_l", k1)
+        d_win = load_words(sb("d_win", [P, G], U32), d_words)
+        x_win = load_words(sb("x_win", [P, T], U32), x_words)
         n2_l = load_list("n2_l", n2)
         n1_l = load_list("n1_l", n1)
         n3_l = load_list("n3_l", n3)
@@ -98,22 +97,30 @@ def tile_picked_hcodeswapderl_none_p_kernel(
         th_c = load_rows("th_c", th)
 
         got1 = sb("got1", [P, H + S], U8)
-        nc.vector.tensor_copy(out=got1[:, :H], in_=d_bytes[:].indirect(k1_l[:]))
         nc.vector.tensor_copy(out=got1[:, H:], in_=x_bytes[:].indirect(offs_l[:]))
+        nc.vector.tensor_copy(out=got1[:, :H], in_=d_bytes[:].indirect(k1_l[:]))
         plane1 = place_scales("plane1", got1, H + S)
         w1_got = sb("w1_got", [P, H], U32)
         nc.vector.tensor_copy(out=w1_got[:], in_=d_win[:].indirect(k1_l[:]))
-        w1 = deal("w1", w1_got[:], U32)
         xq = sb("xq", [P, S], U32)
         nc.vector.tensor_copy(out=xq[:], in_=x_win[:].indirect(offs_l[:]))
-        w1_s = deal("w1_s", plane1[:, :H], U8, tag="x_win")
+        words_by_tile = w1_got[:].rearrange("p (m t) -> p t m", t=PACK)
+        bytes_by_tile = plane1[:, :H].rearrange("p (m t) -> p t m", t=PACK)
 
         h = []
         for t in range(PACK):
             acc = psum.tile([P, S], F32, name=f"acc1_{t}", tag=f"bank{t}")
-            cols = slice(t * P, (t + 1) * P)
+            if t == 0:
+                w1 = sb("w1_first", [P, P], U32)[:]
+            else:
+                if t == 1:
+                    w1_rest = sb("w1_rest", [P, H - P], U32, tag="w1_s0")
+                w1 = w1_rest[:, (t - 1) * P : t * P]
+            w1_s = sb(f"w1_s{t}", [P, P], U8)
+            nc.vector.tensor_copy(out=w1, in_=words_by_tile[:, t, :])
+            nc.vector.tensor_copy(out=w1_s[:], in_=bytes_by_tile[:, t, :])
             nc.tensor.matmul_mx(
-                out=acc[:], lhsT=w1[:, cols].bitcast(FP8X4), lhsT_scale=w1_s[:, cols],
+                out=acc[:], lhsT=w1.bitcast(FP8X4), lhsT_scale=w1_s[:],
                 rhs=xq[:].bitcast(FP8X4), rhs_scale=plane1[:, H:], start=True, stop=True,
             )
             h_t = sb(f"h{t}", [P, S], F32)

from contextlib import ExitStack

import concourse.mybir as mybir

F32 = mybir.dt.float32
BF16 = mybir.dt.bfloat16
I32 = mybir.dt.int32
U32 = mybir.dt.uint32
U16 = mybir.dt.uint16
U8 = mybir.dt.uint8
FP8X4 = mybir.dt.float8_e4m3fn_x4
ALU = mybir.AluOpType
ACT = mybir.ActivationFunctionType

P = 128
PACK = 4
K, T, S, G, H = 512, 1024, 256, 2048, 512
HALF = S // 2
LIST_COL = 16
ROW_STEP = 8
QUAD = 32
FLOPS = 2 * 2 * K * H * S


def tile_picked_hcodeswapderl_none_p_kernel(
    tc, x_words, x_scales, d_words, d_scales, gs, sl, th, offs, k1, n1, n2, n3, k2, n4, n5, out
):
    nc = tc.nc
    with ExitStack() as ctx:
        keep = ctx.enter_context(tc.tile_pool(name="keep", bufs=1))
        psum = ctx.enter_context(tc.psum_pool(name="psum", bufs=1))

        def sb(name, shape, dtype, tag=None):
            return keep.tile(shape, dtype, name=name, tag=tag or name, align_bytes=64)

        def load_list(name, src):
            lst = keep.tile(list(src.shape), U16, name=name)
            nc.sync.dma_start(out=lst[:], in_=src)
            return lst

        def load_scales(name, src, cols):
            win = sb(name, [P, cols], U8)
            rows = src[0].bitcast(I32).unsqueeze(1).to_broadcast([16, ROW_STEP, cols // 4])
            nc.sync.dma_start(out=win[:].bitcast(I32), in_=rows)
            return win

        def load_words(win, src):
            nc.sync.dma_start(out=win[:].bitcast(I32), in_=src[0].rearrange("p c r -> p (c r)").bitcast(I32))
            return win

        def load_rows(name, src):
            col = sb(name, [P, PACK], F32)
            nc.sync.dma_start(out=col[:], in_=src.rearrange("(p t) o -> p (t o)", t=PACK))
            return col

        def half_of(lst, c):
            w = HALF // LIST_COL
            return lst[:, c * w : (c + 1) * w]

        def place_scales(name, got, cols):
            plane = sb(name, [P, cols], U8)
            nc.vector.memset(plane[:].bitcast(I32), 0)
            for q in range(P // QUAD):
                nc.scalar.dma_start(
                    out=plane[QUAD * q : QUAD * q + 4, :].bitcast(I32),
                    in_=got[QUAD * q : QUAD * (q + 1) : ROW_STEP, :].bitcast(I32),
                )
            return plane

        def deal(name, src, dtype, tag=None):
            dealt = sb(name, [P, H], dtype, tag)
            run = 16 if dtype == U8 else 4
            nc.vector.tensor_copy(
                out=dealt[:].rearrange("p (t a b) -> p a t b", t=PACK, b=run),
                in_=src.rearrange("p (a b t) -> p a t b", t=PACK, b=run),
            )
            return dealt

        warm = sb("warm", [P, 16], F32)
        nc.gpsimd.memset(warm[:, 0:1], 0.0)
        nc.scalar.activation(warm[:, 8:9], warm[:, 0:1], ACT.Sigmoid)

        x_bytes = load_scales("x_bytes", x_scales, T)
        offs_l = load_list("offs_l", offs)
        d_bytes = load_scales("d_bytes", d_scales, G)
        k1_l = load_list("k1_l", k1)
        d_win = load_words(sb("d_win", [P, G], U32), d_words)
        x_win = load_words(sb("x_win", [P, T], U32), x_words)
        n2_l = load_list("n2_l", n2)
        n1_l = load_list("n1_l", n1)
        n3_l = load_list("n3_l", n3)
        k2_l = load_list("k2_l", k2)
        n4_l = load_list("n4_l", n4)
        n5_l = load_list("n5_l", n5)
        gs_c = load_rows("gs_c", gs)
        sl_c = load_rows("sl_c", sl)
        th_c = load_rows("th_c", th)

        got1 = sb("got1", [P, H + S], U8)
        nc.vector.tensor_copy(out=got1[:, H:], in_=x_bytes[:].indirect(offs_l[:]))
        nc.vector.tensor_copy(out=got1[:, :H], in_=d_bytes[:].indirect(k1_l[:]))
        plane1 = place_scales("plane1", got1, H + S)
        w1_got = sb("w1_got", [P, H], U32)
        nc.vector.tensor_copy(out=w1_got[:], in_=d_win[:].indirect(k1_l[:]))
        xq = sb("xq", [P, S], U32)
        nc.vector.tensor_copy(out=xq[:], in_=x_win[:].indirect(offs_l[:]))
        words_by_tile = w1_got[:].rearrange("p (m t) -> p t m", t=PACK)
        bytes_by_tile = plane1[:, :H].rearrange("p (m t) -> p t m", t=PACK)

        h = []
        for t in range(PACK):
            acc = psum.tile([P, S], F32, name=f"acc1_{t}", tag=f"bank{t}")
            if t == 0:
                w1 = sb("w1_first", [P, P], U32)[:]
            else:
                if t == 1:
                    w1_rest = sb("w1_rest", [P, H - P], U32, tag="w1_s0")
                w1 = w1_rest[:, (t - 1) * P : t * P]
            w1_s = sb(f"w1_s{t}", [P, P], U8)
            nc.vector.tensor_copy(out=w1, in_=words_by_tile[:, t, :])
            nc.vector.tensor_copy(out=w1_s[:], in_=bytes_by_tile[:, t, :])
            nc.tensor.matmul_mx(
                out=acc[:], lhsT=w1.bitcast(FP8X4), lhsT_scale=w1_s[:],
                rhs=xq[:].bitcast(FP8X4), rhs_scale=plane1[:, H:], start=True, stop=True,
            )
            h_t = sb(f"h{t}", [P, S], F32)
            nc.vector.tensor_scalar_mul(h_t[:], acc[:], 0.0625)
            h.append(h_t)

        bias = sb("bias", [P, PACK], F32)
        nc.vector.scalar_tensor_tensor(out=bias[:], in0=sl_c[:], scalar=-1.0, in1=th_c[:], op0=ALU.mult, op1=ALU.mult)

        dt = [sb(f"dt{t}", [P, S], F32) for t in range(PACK)]
        pb = [sb(f"pb{t}", [P, HALF], F32) for t in range(PACK)]
        rb = [sb(f"rb{t}", [P, HALF], F32) for t in range(PACK)]

        def fetch_pair(t):
            pa = sb(f"pa{t}", [P, HALF], F32)
            nc.scalar.activation(pb[t][:], h[t][:].indirect(n2_l[:]), ACT.Copy)
            nc.scalar.activation(pa[:], h[t][:].indirect(n1_l[:]), ACT.Copy)
            nc.vector.tensor_sub(rb[t][:], pa[:], pb[t][:])

        def put_pb(t):
            nc.scalar.activation(dt[t][:].indirect(n1_l[:]), pb[t][:], ACT.Copy)

        def put_rb(t):
            nc.scalar.activation(dt[t][:].indirect(n2_l[:]), rb[t][:], ACT.Copy)

        def make_z(t, c, other, big):
            nc.scalar.activation(other, dt[t][:].indirect(half_of(n3_l, c)), ACT.Copy)
            nc.vector.scalar_tensor_tensor(
                out=big, in0=other, scalar=0.5, in1=dt[t][:, c * HALF : (c + 1) * HALF], op0=ALU.mult, op1=ALU.max
            )
            nc.vector.tensor_scalar_mul(zb[c][:, :, t], big, gs_c[:, t : t + 1])

        early = sb("early", [P, PACK, HALF], F32)
        fetch_pair(0)
        got2 = sb("got2", [P, H], U8, tag="pa0")
        nc.vector.tensor_copy(out=got2[:], in_=d_bytes[:].indirect(k2_l[:]))
        plane2 = sb("plane2", [P, H], U8)
        nc.vector.memset(plane2[:].bitcast(I32), 0)
        for q in range(P // QUAD):
            nc.sync.dma_start(
                out=plane2[QUAD * q : QUAD * q + 4, :].bitcast(I32),
                in_=got2[QUAD * q : QUAD * (q + 1) : ROW_STEP, :].bitcast(I32),
            )
        w2_s = deal("w2_s", plane2[:], U8)
        big0 = sb("big0", [P, PACK, HALF], F32, tag="plane2")
        put_pb(0)
        fetch_pair(1)
        w2_got = sb("w2_got", [P, H], U32, tag="pa1")
        nc.vector.tensor_copy(out=w2_got[:], in_=d_win[:].indirect(k2_l[:]))
        w2 = deal("w2", w2_got[:], U32)
        zb = [sb("zb0", [P, HALF, PACK], BF16, tag="pa1"), sb("zb1", [P, HALF, PACK], BF16)]
        put_rb(0)
        put_pb(1)
        make_z(0, 0, early[:, 0, :], big0[:, 0, :])
        for t in range(2, PACK):
            fetch_pair(t)
            put_rb(t - 1)
            put_pb(t)
            make_z(t - 1, 0, early[:, t - 1, :], big0[:, t - 1, :])
        put_rb(PACK - 1)
        make_z(PACK - 1, 0, early[:, PACK - 1, :], big0[:, PACK - 1, :])

        h2 = [sb(f"h2_{t}", [P, S], F32) for t in range(PACK)]
        ds2 = [sb(f"ds2_{t}", [P, 2 * S], F32) for t in range(PACK)]

        def second_product(c):
            codes = sb(f"z_codes{c}", [P, HALF], U32)
            scales = sb(f"z_scales{c}", [P, HALF], U8)
            nc.vector.quantize_mx(
                out=codes[:].bitcast(FP8X4), scales=scales[:], in_=zb[c][:].rearrange("p j t -> p (j t)")
            )
            for t in range(PACK):
                acc = psum.tile([P, HALF], F32, name=f"acc2_{t}_{c}", tag=f"bank{PACK * (1 - c) + t}")
                cols = slice(t * P, (t + 1) * P)
                nc.tensor.matmul_mx(
                    out=acc[:], lhsT=w2[:, cols].bitcast(FP8X4), lhsT_scale=w2_s[:, cols],
                    rhs=codes[:].bitcast(FP8X4), rhs_scale=scales[:], start=True, stop=True,
                )
                nc.vector.tensor_scalar_mul(h2[t][:, c * HALF : (c + 1) * HALF], acc[:], 0.0625)

        def put_h2(t, c):
            nc.scalar.activation(ds2[t][:].indirect(half_of(n4_l, c)), h2[t][:, c * HALF : (c + 1) * HALF], ACT.Copy)

        out_rows = out.rearrange("(p t) j -> p t j", t=PACK)

        def finish(t, pieces):
            w = S // pieces
            for c in range(pieces):
                cols = slice(c * w, (c + 1) * w)
                sg = sb(f"sg{t}_{c}", [P, w], F32)
                nc.scalar.activation(
                    sg[:], ds2[t][:].indirect(n5_l[:, c * w // LIST_COL : (c + 1) * w // LIST_COL]), ACT.Sigmoid,
                    bias=bias[:, t : t + 1], scale=sl_c[:, t : t + 1],
                )
                res = sb(f"res{t}_{c}", [P, w], F32)
                nc.vector.tensor_mul(res[:], h2[t][:, cols], sg[:])
                nc.sync.dma_start(out=out_rows[:, t, cols], in_=res[:])

        second_product(0)
        late = sb("late", [P, PACK, HALF], F32, tag=f"rb{PACK - 1}")
        big1 = sb("big1", [P, PACK, HALF], F32, tag="pa1")
        for t in range(PACK):
            make_z(t, 1, late[:, t, :], big1[:, t, :])
        second_product(1)
        for t in range(PACK):
            put_h2(t, 0)
        put_h2(0, 1)
        for t in range(1, PACK):
            put_h2(t, 1)
            finish(t - 1, 1)
        finish(PACK - 1, 2)
